import numpy as np
import ml_dtypes


def mxq(x, axis, fmt="e4m3"):
    dtype, down = {"e4m3": (ml_dtypes.float8_e4m3fn, 7), "e5m2": (ml_dtypes.float8_e5m2, 14)}[fmt]
    v = np.moveaxis(np.asarray(x, np.float32).astype(ml_dtypes.bfloat16).astype(np.float64), axis, -1)
    blocks = v.reshape(v.shape[:-1] + (-1, 32))
    amax = np.abs(blocks).max(-1, keepdims=True)
    byte = np.maximum(np.where(amax > 0, np.frexp(amax)[1] - 1 + 127, 0) - down, 1)
    scale = np.exp2(byte - 127.0)
    codes = (blocks / scale).astype(np.float32).astype(dtype).astype(np.float64)
    return np.moveaxis((codes * scale).reshape(v.shape), -1, axis)


WIDE = False


def mx_kscale(k):
    if not WIDE:
        return np.ones(k)
    levels = np.array([30, -30])
    if k % 512:
        return np.exp2(np.random.permutation(np.resize(levels, k // 32))).repeat(32)
    a = np.empty((k // 512, 16))
    for p in range(k // 512):
        a[p, :8] = np.random.permutation(np.resize(levels, 8))
        for g in range(8):
            far = levels[np.abs(levels - a[p, g]) >= 10]
            a[p, g + 8] = far[np.random.randint(len(far))]
    return np.exp2(a.ravel()).repeat(32)


def f64(x):
    return np.asarray(x).astype(np.float64)


E2M1 = np.array([0.0, 0.5, 1.0, 1.5, 2.0, 3.0, 4.0, 6.0, -0.0, -0.5, -1.0, -1.5, -2.0, -3.0, -4.0, -6.0])


def pack_weight(w, fmt):
    k, n = w.shape
    w = f64(np.asarray(w, np.float32).astype(ml_dtypes.bfloat16)).reshape(k // 32, 32, n)
    amax = np.abs(w).max(1)
    if fmt == "e4m3":
        byte = np.frexp(amax)[1] - 1 + 127 - 7
    else:
        mant, ex = np.frexp(amax / 6.0)
        byte = np.where(mant > 0.5, ex, ex - 1) + 127
    byte = np.clip(np.where(amax > 0, byte, 1), 1, 254)
    scaled = (w * np.exp2(127.0 - byte)[:, None, :]).reshape(k, n).astype(np.float32)
    by_word = np.ascontiguousarray(scaled.reshape(k // 512, 128, 4, n).transpose(0, 1, 3, 2))
    if fmt == "e4m3":
        words = by_word.astype(ml_dtypes.float8_e4m3fn).view(np.uint8)
    else:
        c = by_word.astype(ml_dtypes.float4_e2m1fn).view(np.uint8) & 0xF
        words = (c[..., 0::2] | (c[..., 1::2] << 4)).reshape(k // 512, 128, 2 * n)
    return np.ascontiguousarray(words), np.ascontiguousarray(byte.astype(np.uint8).reshape(k // 512, 16, n))


def unpack_weight(words, scales, fmt):
    g, _, n = scales.shape
    words = np.ascontiguousarray(words).reshape(g, 128, n, -1)
    if fmt == "e4m3":
        vals = words.view(ml_dtypes.float8_e4m3fn).astype(np.float64)
    else:
        nib = np.empty((g, 128, n, 4), np.uint8)
        nib[..., 0::2] = words & 0xF
        nib[..., 1::2] = words >> 4
        vals = E2M1[nib]
    vals = vals * np.repeat(np.exp2(scales.astype(np.float64) - 127.0), 8, axis=1)[..., None]
    return vals.transpose(0, 1, 3, 2).reshape(g * 512, n)


def bf(x):
    return np.asarray(x, np.float32).astype(ml_dtypes.bfloat16)


def planes(Y):
    r, m = Y.shape
    b = f64(bf(Y)).reshape(r // 32, 32, m)
    amax = np.abs(b).max(1)
    byte = np.clip(np.where(amax > 0, np.frexp(amax)[1] - 1 + 127 - 7, 1), 1, 254)
    codes = (b * np.exp2(127.0 - byte)[:, None, :]).reshape(r, m).astype(np.float32).astype(ml_dtypes.float8_e4m3fn).view(np.uint8)
    words = codes.reshape(r // 512, 128, 4, m).transpose(0, 1, 3, 2)
    return np.ascontiguousarray(words), np.ascontiguousarray(byte.astype(np.uint8).reshape(r // 512, 16, m))


K, L, M, T, N = 512, 512, 512, 512, 512


def setup_inputs():
    n = np.random.standard_normal
    fk = mx_kscale(K)
    fl = mx_kscale(L)
    fm = mx_kscale(M)
    xtp = pack_weight(n((K, T)) / fk[:, None], "e2m1")
    wap = pack_weight(n((K, M)) * 1 / np.sqrt(K) * fk[:, None], "e4m3")
    xqp = pack_weight(n((L, T)) / fl[:, None], "e2m1")
    wcp = pack_weight(n((L, M)) * 1 / np.sqrt(L) * fl[:, None], "e4m3")
    wbp = pack_weight(n((K, M)) * 1 / np.sqrt(K) * fk[:, None], "e4m3")
    wep = pack_weight(n((L, M)) * 1 / np.sqrt(L) * fl[:, None], "e2m1")
    wtp = pack_weight(n((M, N)) * 1 / np.sqrt(M) / fm[:, None], "e4m3")
    return {
        "xt_words": xtp[0],
        "xt_scales": xtp[1],
        "wa_words": wap[0],
        "wa_scales": wap[1],
        "xq_words": xqp[0],
        "xq_scales": xqp[1],
        "wc_words": wcp[0],
        "wc_scales": wcp[1],
        "wb_words": wbp[0],
        "wb_scales": wbp[1],
        "we_words": wep[0],
        "we_scales": wep[1],
        "us": (np.random.uniform(0.5, 2.0, (M, 1)) * fm[:, None]).astype(np.float32),
        "wt_words": wtp[0],
        "wt_scales": wtp[1],
        "rw": (np.random.uniform(0.5, 2.0, (1, T))).astype(np.float32),
    }


def reference(xt_words, xt_scales, wa_words, wa_scales, xq_words, xq_scales, wc_words, wc_scales, wb_words, wb_scales, we_words, we_scales, us, wt_words, wt_scales, rw):
    xtu = unpack_weight(xt_words, xt_scales, "e2m1")
    wau = unpack_weight(wa_words, wa_scales, "e4m3")
    xqu = unpack_weight(xq_words, xq_scales, "e2m1")
    wcu = unpack_weight(wc_words, wc_scales, "e4m3")
    wbu = unpack_weight(wb_words, wb_scales, "e4m3")
    weu = unpack_weight(we_words, we_scales, "e2m1")
    wtu = unpack_weight(wt_words, wt_scales, "e4m3")
    p = wau.T @ xtu + wcu.T @ xqu
    q = wbu.T @ xtu + weu.T @ xqu
    d = np.tanh(p - q) * f64(us)
    dq = mxq(d, 0, "e5m2")
    b = wtu.T @ dq
    y = b * f64(rw)
    words, scales = planes(y)
    return y, words, scales

@@ -1,0 +1,223 @@
+from contextlib import ExitStack
+
+import concourse.mybir as mybir
+from concourse.masks import make_identity
+
+K = L = M = T = N = 512
+FLOPS = 2 * (2 * K * M * T + 2 * L * M * T + M * N * T)
+
+F32 = mybir.dt.float32
+BF16 = mybir.dt.bfloat16
+I32 = mybir.dt.int32
+U8 = mybir.dt.uint8
+E4M3 = mybir.dt.float8_e4m3fn_x4
+E5M2 = mybir.dt.float8_e5m2_x4
+E2M1 = mybir.dt.float4_e2m1fn_x4
+ACT = mybir.ActivationFunctionType
+ALU = mybir.AluOpType
+
+P = 128
+PACK = 4
+TILES = T // P
+QUADS = 4
+HALF = T // 2
+SPLIT = 144
+
+
+def tile_mix_gap_of_two_sums_back_pl_kernel(
+    tc, xt_words, xt_scales, wa_words, wa_scales, xq_words, xq_scales, wc_words, wc_scales,
+    wb_words, wb_scales, we_words, we_scales, us, wt_words, wt_scales, rw, out_0, out_1, out_2,
+):
+    nc = tc.nc
+    with ExitStack() as ctx:
+        sb = ctx.enter_context(tc.tile_pool(name="sb", bufs=1))
+        ps = ctx.enter_context(tc.psum_pool(name="ps", bufs=1))
+        ctx.enter_context(tc.manual_schedule())
+
+        def new_plane(name, engine):
+            plane = sb.tile([P, 512], U8, name=name, align_bytes=64)
+            engine.memset(plane[:].bitcast(I32), 0)
+            return plane
+
+        def load_words(name, words, queue):
+            flat = words[0] if len(words.shape) == 3 else words[0].rearrange("p c r -> p (c r)")
+            tile = sb.tile([P, flat.shape[1]], U8, name=name, align_bytes=64)
+            queue.dma_start(out=tile[:].bitcast(I32), in_=flat.bitcast(I32))
+            return tile
+
+        def load_scales(plane, scales, queues):
+            for q in range(QUADS):
+                queues[q].dma_start(
+                    out=plane[32 * q : 32 * q + 4, :].bitcast(I32),
+                    in_=scales[0, 4 * q : 4 * q + 4, :].bitcast(I32),
+                )
+
+        planes = sb.tile([P, 6 * 512], U8, name="planes", align_bytes=64)
+        nc.vector.memset(planes[:].bitcast(I32), 0)
+        wt_s = new_plane("wt_s", nc.vector)
+        staged = sb.tile([P, 6 * 512], U8, name="staged", align_bytes=64)
+        d_w = sb.tile([P, HALF + T], I32, name="d_w", align_bytes=64)
+        d_s = sb.tile([P, HALF + T], U8, name="d_s", align_bytes=64)
+        nc.vector.memset(d_w[:, 0:HALF], 0)
+        nc.vector.memset(d_s[:, 0:HALF].bitcast(I32), 0)
+        on_sync = [nc.sync] * QUADS
+        both = [nc.sync, nc.scalar]
+        for o, scales in enumerate([xt_scales, wb_scales, xq_scales, we_scales, wa_scales, wc_scales]):
+            both[o % 2].dma_start(
+                out=staged[0:P:8, 512 * o : 512 * (o + 1)].bitcast(I32), in_=scales[0].bitcast(I32)
+            )
+        xt_s, wb_s, xq_s, we_s, wa_s, wc_s = [planes[:, 512 * o : 512 * (o + 1)] for o in range(6)]
+        xt_w = load_words("xt_w", xt_words, nc.sync)
+        wb_w = load_words("wb_w", wb_words, nc.scalar)
+        xq_w = load_words("xq_w", xq_words, nc.scalar)
+        we_w = load_words("we_w", we_words, nc.scalar)
+        for r in range(4):
+            nc.sync.dma_start(out=planes[r:P:32, :].bitcast(I32), in_=staged[8 * r : P : 32, :].bitcast(I32))
+        wa_w = load_words("wa_w", wa_words, nc.sync)
+        wc_w = load_words("wc_w", wc_words, nc.sync)
+        wt_w = load_words("wt_w", wt_words, nc.sync)
+        load_scales(wt_s, wt_scales, on_sync)
+        us_sb = sb.tile([P, PACK], F32, name="us_sb")
+        nc.sync.dma_start(out=us_sb[:], in_=us.rearrange("(p j) o -> p (j o)", j=PACK))
+        rw_sb = sb.tile([P, T], F32, name="rw_sb")
+        nc.sync.dma_start(out=rw_sb[:], in_=rw[0].partition_broadcast(P))
+
+        ident = sb.tile([P, P], F32, name="ident")
+        make_identity(nc, ident[:])
+        wt_sd = sb.tile([P, N], U8, name="wt_sd", align_bytes=64)
+        nc.gpsimd.tensor_copy(
+            out=wt_sd[:].rearrange("p (i c) -> p i c", i=PACK),
+            in_=wt_s[:].rearrange("p (c i) -> p i c", i=PACK),
+        )
+        wt_wd = sb.tile([P, N], I32, name="wt_wd", align_bytes=64)
+        nc.gpsimd.tensor_copy(
+            out=wt_wd[:].rearrange("p (i c) -> p i c", i=PACK),
+            in_=wt_w[:].bitcast(I32).rearrange("p (c i) -> p i c", i=PACK),
+        )
+
+        def product(bank, x_w, x_s, a, w_w, w_s, w_fmt, first):
+            nc.tensor.matmul_mx(
+                out=bank[:],
+                lhsT=x_w[:, 2 * P * a : 2 * P * (a + 1)].bitcast(E2M1),
+                lhsT_scale=x_s[:, P * a : P * (a + 1)],
+                rhs=w_w[:].bitcast(w_fmt),
+                rhs_scale=w_s,
+                start=first,
+                stop=not first,
+            )
+
+        q_ps = [ps.tile([P, M], F32, name="q_ps%d" % a, tag="bank%d" % a) for a in range(TILES)]
+        p_ps = [ps.tile([P, M], F32, name="p_ps%d" % a, tag="bank%d" % (TILES + a)) for a in range(TILES)]
+        for a in range(TILES):
+            product(q_ps[a], xt_w, xt_s, a, wb_w, wb_s, E4M3, True)
+            product(q_ps[a], xq_w, xq_s, a, we_w, we_s, E2M1, False)
+            product(p_ps[a], xt_w, xt_s, a, wa_w, wa_s, E4M3, True)
+            product(p_ps[a], xq_w, xq_s, a, wc_w, wc_s, E4M3, False)
+
+        q_sb = [sb.tile([P, PACK, P], F32, name="q_sb%d" % a) for a in range(TILES)]
+        gap = [sb.tile([P, PACK, P], F32, name="gap%d" % a) for a in range(TILES)]
+        th = [sb.tile([P, PACK, P], F32, name="th%d" % a) for a in range(TILES)]
+
+        def copy_q(a):
+            nc.scalar.activation(out=q_sb[a][:], in_=q_ps[a][:].rearrange("t (c j) -> t j c", j=PACK), func=ACT.Copy)
+
+        copy_q(0)
+        for a in range(TILES):
+            if a + 1 < TILES:
+                copy_q(a + 1)
+            nc.vector.tensor_tensor(
+                out=gap[a][:], in0=p_ps[a][:].rearrange("t (c j) -> t j c", j=PACK), in1=q_sb[a][:], op=ALU.subtract
+            )
+            nc.scalar.activation(out=th[a][:], in_=gap[a][:], func=ACT.Tanh)
+
+        d_bf = [sb.tile([P, P, PACK], BF16, name="d_bf%d" % a, align_bytes=64) for a in range(TILES)]
+
+        def quantise_d(a):
+            nc.vector.quantize_mx(
+                out=d_w[:, HALF + P * a : HALF + P * (a + 1)].bitcast(E5M2),
+                scales=d_s[:, HALF + P * a : HALF + P * (a + 1)],
+                in_=d_bf[a][:].rearrange("p t j -> p (t j)"),
+            )
+
+        turned = [ps.tile([P, PACK, P], F32, name="turned%d" % a, tag="bank%d" % a) for a in range(TILES)]
+        for a in range(TILES):
+            for j in range(PACK):
+                nc.tensor.transpose(turned[a][:, j, :], th[a][:, j, :], ident[:])
+
+        def weigh(a):
+            nc.vector.tensor_tensor(
+                out=d_bf[a][:],
+                in0=turned[a][:].rearrange("p j t -> p t j"),
+                in1=us_sb[:].unsqueeze(1).to_broadcast([P, P, PACK]),
+                op=ALU.mult,
+            )
+
+        y = [sb.tile([P, PACK, HALF], F32, name="y%d" % h) for h in range(2)]
+        y_bf = sb.tile([P, T, PACK], BF16, name="y_bf", align_bytes=64)
+        y_w = sb.tile([P, T], I32, name="y_w", align_bytes=64)
+        y_s = sb.tile([P, T], U8, name="y_s", align_bytes=64)
+        out_rows = out_0.rearrange("(p i) t -> p i t", i=PACK)
+
+        def way_back(h):
+            banks = []
+            for i in range(PACK):
+                b_ps = ps.tile([P, T], F32, name="b_ps%d_%d" % (h, i), tag="bank%d" % (TILES * (1 - h) + i))
+                nc.tensor.matmul_mx(
+                    out=b_ps[:],
+                    lhsT=wt_wd[:, P * i : P * (i + 1)].bitcast(E4M3),
+                    lhsT_scale=wt_sd[:, P * i : P * (i + 1)],
+                    rhs=d_w[:, HALF * h : HALF * h + T].bitcast(E5M2),
+                    rhs_scale=d_s[:, HALF * h : HALF * h + T],
+                    start=True,
+                    stop=True,
+                )
+                banks.append(b_ps)
+            return banks
+
+        def results(h, banks):
+            cols = slice(HALF * h, HALF * (h + 1))
+            for i in range(PACK):
+                nc.vector.tensor_tensor(out=y[h][:, i, :], in0=banks[i][:, HALF:T], in1=rw_sb[:, cols], op=ALU.mult)
+                if i % 2 == 1:
+                    nc.sync.dma_start(out=out_rows[:, i - 1 : i + 1, cols], in_=y[h][:, i - 1 : i + 1, :])
+
+        def interleave(copy, h, t0, t1):
+            copy(
+                out=y_bf[:, HALF * h + t0 : HALF * h + t1, :].rearrange("p (c e) i -> p c i e", e=4),
+                in_=y[h][:, :, t0:t1].rearrange("p i (c e) -> p c i e", e=4),
+            )
+
+        def quantise_y(h):
+            cols = slice(HALF * h, HALF * (h + 1))
+            nc.vector.quantize_mx(
+                out=y_w[:, cols].bitcast(E4M3),
+                scales=y_s[:, cols],
+                in_=y_bf[:, cols, :].rearrange("p t i -> p (t i)"),
+            )
+            nc.sync.dma_start(
+                out=out_1[0].rearrange("p c r -> p (c r)").bitcast(I32)[:, cols], in_=y_w[:, cols]
+            )
+
+        weigh(0)
+        weigh(1)
+        quantise_d(0)
+        quantise_d(1)
+        first = way_back(0)
+        weigh(2)
+        weigh(3)
+        quantise_d(2)
+        quantise_d(3)
+        second = way_back(1)
+        results(0, first)
+        interleave(nc.scalar.copy, 0, 0, HALF)
+        results(1, second)
+        interleave(nc.scalar.copy, 1, SPLIT, HALF)
+        interleave(nc.vector.tensor_copy, 1, 0, SPLIT)
+        quantise_y(0)
+        quantise_y(1)
+        for q in range(QUADS):
+            queue = nc.scalar if q % 2 == 0 else nc.sync
+            queue.dma_start(
+                out=out_2[0, 4 * q : 4 * q + 4, :].bitcast(I32),
+                in_=y_s[32 * q : 32 * q + 4, :].bitcast(I32),
+            )

@@ -22,6 +22,7 @@ TILES = T // P
 QUADS = 4
 HALF = T // 2
 SPLIT = 144
+WARM_PASSES = 3
 
 
 def tile_mix_gap_of_two_sums_back_pl_kernel(
@@ -52,19 +53,21 @@ def tile_mix_gap_of_two_sums_back_pl_kernel(
                     in_=scales[0, 4 * q : 4 * q + 4, :].bitcast(I32),
                 )
 
+        staged = sb.tile([P, 6 * 512], U8, name="staged", align_bytes=64)
+        nc.vector.memset(staged[:, 0:512].bitcast(I32), 0)
         planes = sb.tile([P, 6 * 512], U8, name="planes", align_bytes=64)
         nc.vector.memset(planes[:].bitcast(I32), 0)
         wt_s = new_plane("wt_s", nc.vector)
-        staged = sb.tile([P, 6 * 512], U8, name="staged", align_bytes=64)
         d_w = sb.tile([P, HALF + T], I32, name="d_w", align_bytes=64)
         d_s = sb.tile([P, HALF + T], U8, name="d_s", align_bytes=64)
         nc.vector.memset(d_w[:, 0:HALF], 0)
         nc.vector.memset(d_s[:, 0:HALF].bitcast(I32), 0)
         on_sync = [nc.sync] * QUADS
         both = [nc.sync, nc.scalar]
-        for o, scales in enumerate([xt_scales, wb_scales, xq_scales, we_scales, wa_scales, wc_scales]):
+        all_scales = [xt_scales, wb_scales, xq_scales, we_scales, wa_scales, wc_scales]
+        for o in reversed(range(6)):
             both[o % 2].dma_start(
-                out=staged[0:P:8, 512 * o : 512 * (o + 1)].bitcast(I32), in_=scales[0].bitcast(I32)
+                out=staged[0:P:8, 512 * o : 512 * (o + 1)].bitcast(I32), in_=all_scales[o][0].bitcast(I32)
             )
         xt_s, wb_s, xq_s, we_s, wa_s, wc_s = [planes[:, 512 * o : 512 * (o + 1)] for o in range(6)]
         xt_w = load_words("xt_w", xt_words, nc.sync)
@@ -84,16 +87,13 @@ def tile_mix_gap_of_two_sums_back_pl_kernel(
 
         ident = sb.tile([P, P], F32, name="ident")
         make_identity(nc, ident[:])
-        wt_sd = sb.tile([P, N], U8, name="wt_sd", align_bytes=64)
-        nc.gpsimd.tensor_copy(
-            out=wt_sd[:].rearrange("p (i c) -> p i c", i=PACK),
-            in_=wt_s[:].rearrange("p (c i) -> p i c", i=PACK),
-        )
         wt_wd = sb.tile([P, N], I32, name="wt_wd", align_bytes=64)
-        nc.gpsimd.tensor_copy(
-            out=wt_wd[:].rearrange("p (i c) -> p i c", i=PACK),
-            in_=wt_w[:].bitcast(I32).rearrange("p (c i) -> p i c", i=PACK),
-        )
+        wt_sd = sb.tile([P, N], U8, name="wt_sd", align_bytes=64)
+
+        def deal(dealt, natural):
+            nc.vector.tensor_copy(
+                out=dealt.rearrange("p (i c) -> p c i", i=PACK), in_=natural.rearrange("p (c i) -> p c i", i=PACK)
+            )
 
         def product(bank, x_w, x_s, a, w_w, w_s, w_fmt, first):
             nc.tensor.matmul_mx(
@@ -106,31 +106,53 @@ def tile_mix_gap_of_two_sums_back_pl_kernel(
                 stop=not first,
             )
 
-        q_ps = [ps.tile([P, M], F32, name="q_ps%d" % a, tag="bank%d" % a) for a in range(TILES)]
-        p_ps = [ps.tile([P, M], F32, name="p_ps%d" % a, tag="bank%d" % (TILES + a)) for a in range(TILES)]
-        for a in range(TILES):
+        warm = ps.tile([P, M], F32, name="warm", tag="bank7")
+        for rehearsal in range(WARM_PASSES):
+            nc.tensor.matmul_mx(
+                out=warm[:],
+                lhsT=xt_w[:, 0 : 2 * P].bitcast(E2M1),
+                lhsT_scale=staged[:, 0:P],
+                rhs=xt_w[:].bitcast(E2M1),
+                rhs_scale=staged[:, 0:T],
+                start=True,
+                stop=True,
+            )
+
+        q_ps, p_ps, q_sb, th, turned, d_bf, b_ps = {}, {}, {}, {}, {}, {}, {}
+
+        def sums(a):
+            q_ps[a] = ps.tile([P, M], F32, name="q_ps%d" % a, tag="bank%d" % a)
+            p_ps[a] = ps.tile([P, M], F32, name="p_ps%d" % a, tag="bank%d" % (TILES + a))
             product(q_ps[a], xt_w, xt_s, a, wb_w, wb_s, E4M3, True)
             product(q_ps[a], xq_w, xq_s, a, we_w, we_s, E2M1, False)
             product(p_ps[a], xt_w, xt_s, a, wa_w, wa_s, E4M3, True)
             product(p_ps[a], xq_w, xq_s, a, wc_w, wc_s, E4M3, False)
 
-        q_sb = [sb.tile([P, PACK, P], F32, name="q_sb%d" % a) for a in range(TILES)]
-        gap = [sb.tile([P, PACK, P], F32, name="gap%d" % a) for a in range(TILES)]
-        th = [sb.tile([P, PACK, P], F32, name="th%d" % a) for a in range(TILES)]
-
         def copy_q(a):
+            q_sb[a] = sb.tile([P, PACK, P], F32, name="q_sb%d" % a)
             nc.scalar.activation(out=q_sb[a][:], in_=q_ps[a][:].rearrange("t (c j) -> t j c", j=PACK), func=ACT.Copy)
 
-        copy_q(0)
-        for a in range(TILES):
-            if a + 1 < TILES:
-                copy_q(a + 1)
+        def tanh_of_gap(a):
+            gap = sb.tile([P, PACK, P], F32, name="gap%d" % a)
             nc.vector.tensor_tensor(
-                out=gap[a][:], in0=p_ps[a][:].rearrange("t (c j) -> t j c", j=PACK), in1=q_sb[a][:], op=ALU.subtract
+                out=gap[:], in0=p_ps[a][:].rearrange("t (c j) -> t j c", j=PACK), in1=q_sb[a][:], op=ALU.subtract
             )
-            nc.scalar.activation(out=th[a][:], in_=gap[a][:], func=ACT.Tanh)
+            th[a] = sb.tile([P, PACK, P], F32, name="th%d" % a)
+            nc.scalar.activation(out=th[a][:], in_=gap[:], func=ACT.Tanh)
 
-        d_bf = [sb.tile([P, P, PACK], BF16, name="d_bf%d" % a, align_bytes=64) for a in range(TILES)]
+        def turn(a):
+            turned[a] = ps.tile([P, PACK, P], F32, name="turned%d" % a, tag="bank%d" % a)
+            for j in range(PACK):
+                nc.tensor.transpose(turned[a][:, j, :], th[a][:, j, :], ident[:])
+
+        def weigh(a):
+            d_bf[a] = sb.tile([P, P, PACK], BF16, name="d_bf%d" % a, align_bytes=64)
+            nc.vector.tensor_tensor(
+                out=d_bf[a][:],
+                in0=turned[a][:].rearrange("p j t -> p t j"),
+                in1=us_sb[:].unsqueeze(1).to_broadcast([P, P, PACK]),
+                op=ALU.mult,
+            )
 
         def quantise_d(a):
             nc.vector.quantize_mx(
@@ -139,47 +161,29 @@ def tile_mix_gap_of_two_sums_back_pl_kernel(
                 in_=d_bf[a][:].rearrange("p t j -> p (t j)"),
             )
 
-        turned = [ps.tile([P, PACK, P], F32, name="turned%d" % a, tag="bank%d" % a) for a in range(TILES)]
-        for a in range(TILES):
-            for j in range(PACK):
-                nc.tensor.transpose(turned[a][:, j, :], th[a][:, j, :], ident[:])
-
-        def weigh(a):
-            nc.vector.tensor_tensor(
-                out=d_bf[a][:],
-                in0=turned[a][:].rearrange("p j t -> p t j"),
-                in1=us_sb[:].unsqueeze(1).to_broadcast([P, P, PACK]),
-                op=ALU.mult,
-            )
-
         y = [sb.tile([P, PACK, HALF], F32, name="y%d" % h) for h in range(2)]
         y_bf = sb.tile([P, T, PACK], BF16, name="y_bf", align_bytes=64)
         y_w = sb.tile([P, T], I32, name="y_w", align_bytes=64)
         y_s = sb.tile([P, T], U8, name="y_s", align_bytes=64)
         out_rows = out_0.rearrange("(p i) t -> p i t", i=PACK)
 
-        def way_back(h):
-            banks = []
-            for i in range(PACK):
-                b_ps = ps.tile([P, T], F32, name="b_ps%d_%d" % (h, i), tag="bank%d" % (TILES * (1 - h) + i))
-                nc.tensor.matmul_mx(
-                    out=b_ps[:],
-                    lhsT=wt_wd[:, P * i : P * (i + 1)].bitcast(E4M3),
-                    lhsT_scale=wt_sd[:, P * i : P * (i + 1)],
-                    rhs=d_w[:, HALF * h : HALF * h + T].bitcast(E5M2),
-                    rhs_scale=d_s[:, HALF * h : HALF * h + T],
-                    start=True,
-                    stop=True,
-                )
-                banks.append(b_ps)
-            return banks
+        def way_back(h, i):
+            b_ps[h, i] = ps.tile([P, T], F32, name="b_ps%d_%d" % (h, i), tag="bank%d" % (TILES * (1 - h) + i))
+            nc.tensor.matmul_mx(
+                out=b_ps[h, i][:],
+                lhsT=wt_wd[:, P * i : P * (i + 1)].bitcast(E4M3),
+                lhsT_scale=wt_sd[:, P * i : P * (i + 1)],
+                rhs=d_w[:, HALF * h : HALF * h + T].bitcast(E5M2),
+                rhs_scale=d_s[:, HALF * h : HALF * h + T],
+                start=True,
+                stop=True,
+            )
 
-        def results(h, banks):
+        def result(h, i):
             cols = slice(HALF * h, HALF * (h + 1))
-            for i in range(PACK):
-                nc.vector.tensor_tensor(out=y[h][:, i, :], in0=banks[i][:, HALF:T], in1=rw_sb[:, cols], op=ALU.mult)
-                if i % 2 == 1:
-                    nc.sync.dma_start(out=out_rows[:, i - 1 : i + 1, cols], in_=y[h][:, i - 1 : i + 1, :])
+            nc.vector.tensor_tensor(out=y[h][:, i, :], in0=b_ps[h, i][:, HALF:T], in1=rw_sb[:, cols], op=ALU.mult)
+            if i % 2 == 1:
+                nc.sync.dma_start(out=out_rows[:, i - 1 : i + 1, cols], in_=y[h][:, i - 1 : i + 1, :])
 
         def interleave(copy, h, t0, t1):
             copy(
@@ -187,36 +191,49 @@ def tile_mix_gap_of_two_sums_back_pl_kernel(
                 in_=y[h][:, :, t0:t1].rearrange("p i (c e) -> p c i e", e=4),
             )
 
-        def quantise_y(h):
+        def quantise_y(h, queue):
             cols = slice(HALF * h, HALF * (h + 1))
             nc.vector.quantize_mx(
                 out=y_w[:, cols].bitcast(E4M3),
                 scales=y_s[:, cols],
                 in_=y_bf[:, cols, :].rearrange("p t i -> p (t i)"),
             )
-            nc.sync.dma_start(
-                out=out_1[0].rearrange("p c r -> p (c r)").bitcast(I32)[:, cols], in_=y_w[:, cols]
-            )
+            queue.dma_start(out=out_1[0].rearrange("p c r -> p (c r)").bitcast(I32)[:, cols], in_=y_w[:, cols])
 
-        weigh(0)
-        weigh(1)
-        quantise_d(0)
-        quantise_d(1)
-        first = way_back(0)
-        weigh(2)
-        weigh(3)
-        quantise_d(2)
-        quantise_d(3)
-        second = way_back(1)
-        results(0, first)
+        sums(0)
+        copy_q(0)
+        sums(1)
+        copy_q(1)
+        tanh_of_gap(0)
+        deal(wt_wd[:], wt_w[:].bitcast(I32))
+        sums(2)
+        copy_q(2)
+        tanh_of_gap(1)
+        deal(wt_sd[:], wt_s[:])
+        sums(3)
+        copy_q(3)
+        tanh_of_gap(2)
+        tanh_of_gap(3)
+        for a in range(TILES):
+            turn(a)
+        for h in range(2):
+            weigh(2 * h)
+            weigh(2 * h + 1)
+            quantise_d(2 * h)
+            quantise_d(2 * h + 1)
+            for i in range(PACK):
+                way_back(h, i)
+        for i in range(PACK):
+            result(0, i)
         interleave(nc.scalar.copy, 0, 0, HALF)
-        results(1, second)
+        for i in range(PACK):
+            result(1, i)
         interleave(nc.scalar.copy, 1, SPLIT, HALF)
         interleave(nc.vector.tensor_copy, 1, 0, SPLIT)
-        quantise_y(0)
-        quantise_y(1)
+        quantise_y(0, nc.sync)
+        quantise_y(1, nc.scalar)
         for q in range(QUADS):
-            queue = nc.scalar if q % 2 == 0 else nc.sync
+            queue = nc.scalar if q == 0 else nc.sync
             queue.dma_start(
                 out=out_2[0, 4 * q : 4 * q + 4, :].bitcast(I32),
                 in_=y_s[32 * q : 32 * q + 4, :].bitcast(I32),

@@ -154,6 +154,13 @@ def tile_mix_gap_of_two_sums_back_pl_kernel(
                 op=ALU.mult,
             )
 
+        def weigh_on_scalar(a):
+            d_bf[a] = sb.tile([P, P, PACK], BF16, name="d_bf%d" % a, align_bytes=64)
+            for j in range(PACK):
+                nc.scalar.activation(
+                    out=d_bf[a][:, :, j], in_=turned[a][:, j, :], func=ACT.Copy, scale=us_sb[:, j : j + 1]
+                )
+
         def quantise_d(a):
             nc.vector.quantize_mx(
                 out=d_w[:, HALF + P * a : HALF + P * (a + 1)].bitcast(E5M2),
@@ -216,15 +223,21 @@ def tile_mix_gap_of_two_sums_back_pl_kernel(
         tanh_of_gap(3)
         for a in range(TILES):
             turn(a)
-        for h in range(2):
-            weigh(2 * h)
-            weigh(2 * h + 1)
-            quantise_d(2 * h)
-            quantise_d(2 * h + 1)
-            for i in range(PACK):
-                way_back(h, i)
+        weigh_on_scalar(2)
+        weigh(0)
+        weigh(1)
+        quantise_d(0)
+        quantise_d(1)
         for i in range(PACK):
+            way_back(0, i)
+        weigh(3)
+        result(0, 0)
+        quantise_d(3)
+        quantise_d(2)
+        for i in range(1, PACK):
             result(0, i)
+        for i in range(PACK):
+            way_back(1, i)
         interleave(nc.scalar.copy, 0, 0, HALF)
         for i in range(PACK):
             result(1, i)

from contextlib import ExitStack

import concourse.mybir as mybir
from concourse.masks import make_identity

K = L = M = T = N = 512
FLOPS = 2 * (2 * K * M * T + 2 * L * M * T + M * N * T)

F32 = mybir.dt.float32
BF16 = mybir.dt.bfloat16
I32 = mybir.dt.int32
U8 = mybir.dt.uint8
E4M3 = mybir.dt.float8_e4m3fn_x4
E5M2 = mybir.dt.float8_e5m2_x4
E2M1 = mybir.dt.float4_e2m1fn_x4
ACT = mybir.ActivationFunctionType
ALU = mybir.AluOpType

P = 128
PACK = 4
TILES = T // P
QUADS = 4
HALF = T // 2
SPLIT = 144
WARM_PASSES = 3


def tile_mix_gap_of_two_sums_back_pl_kernel(
    tc, xt_words, xt_scales, wa_words, wa_scales, xq_words, xq_scales, wc_words, wc_scales,
    wb_words, wb_scales, we_words, we_scales, us, wt_words, wt_scales, rw, out_0, out_1, out_2,
):
    nc = tc.nc
    with ExitStack() as ctx:
        sb = ctx.enter_context(tc.tile_pool(name="sb", bufs=1))
        ps = ctx.enter_context(tc.psum_pool(name="ps", bufs=1))
        ctx.enter_context(tc.manual_schedule())

        def new_plane(name, engine):
            plane = sb.tile([P, 512], U8, name=name, align_bytes=64)
            engine.memset(plane[:].bitcast(I32), 0)
            return plane

        def load_words(name, words, queue):
            flat = words[0] if len(words.shape) == 3 else words[0].rearrange("p c r -> p (c r)")
            tile = sb.tile([P, flat.shape[1]], U8, name=name, align_bytes=64)
            queue.dma_start(out=tile[:].bitcast(I32), in_=flat.bitcast(I32))
            return tile

        def load_scales(plane, scales, queues):
            for q in range(QUADS):
                queues[q].dma_start(
                    out=plane[32 * q : 32 * q + 4, :].bitcast(I32),
                    in_=scales[0, 4 * q : 4 * q + 4, :].bitcast(I32),
                )

        staged = sb.tile([P, 6 * 512], U8, name="staged", align_bytes=64)
        nc.vector.memset(staged[:, 0:512].bitcast(I32), 0)
        planes = sb.tile([P, 6 * 512], U8, name="planes", align_bytes=64)
        nc.vector.memset(planes[:].bitcast(I32), 0)
        wt_s = new_plane("wt_s", nc.vector)
        d_w = sb.tile([P, HALF + T], I32, name="d_w", align_bytes=64)
        d_s = sb.tile([P, HALF + T], U8, name="d_s", align_bytes=64)
        nc.vector.memset(d_w[:, 0:HALF], 0)
        nc.vector.memset(d_s[:, 0:HALF].bitcast(I32), 0)
        on_sync = [nc.sync] * QUADS
        both = [nc.sync, nc.scalar]
        all_scales = [xt_scales, wb_scales, xq_scales, we_scales, wa_scales, wc_scales]
        for o in reversed(range(6)):
            both[o % 2].dma_start(
                out=staged[0:P:8, 512 * o : 512 * (o + 1)].bitcast(I32), in_=all_scales[o][0].bitcast(I32)
            )
        xt_s, wb_s, xq_s, we_s, wa_s, wc_s = [planes[:, 512 * o : 512 * (o + 1)] for o in range(6)]
        xt_w = load_words("xt_w", xt_words, nc.sync)
        wb_w = load_words("wb_w", wb_words, nc.scalar)
        xq_w = load_words("xq_w", xq_words, nc.scalar)
        we_w = load_words("we_w", we_words, nc.scalar)
        for r in range(4):
            nc.sync.dma_start(out=planes[r:P:32, :].bitcast(I32), in_=staged[8 * r : P : 32, :].bitcast(I32))
        wa_w = load_words("wa_w", wa_words, nc.sync)
        wc_w = load_words("wc_w", wc_words, nc.sync)
        wt_w = load_words("wt_w", wt_words, nc.sync)
        load_scales(wt_s, wt_scales, on_sync)
        us_sb = sb.tile([P, PACK], F32, name="us_sb")
        nc.sync.dma_start(out=us_sb[:], in_=us.rearrange("(p j) o -> p (j o)", j=PACK))
        rw_sb = sb.tile([P, T], F32, name="rw_sb")
        nc.sync.dma_start(out=rw_sb[:], in_=rw[0].partition_broadcast(P))

        ident = sb.tile([P, P], F32, name="ident")
        make_identity(nc, ident[:])
        wt_wd = sb.tile([P, N], I32, name="wt_wd", align_bytes=64)
        wt_sd = sb.tile([P, N], U8, name="wt_sd", align_bytes=64)

        def deal(dealt, natural):
            nc.vector.tensor_copy(
                out=dealt.rearrange("p (i c) -> p c i", i=PACK), in_=natural.rearrange("p (c i) -> p c i", i=PACK)
            )

        def product(bank, x_w, x_s, a, w_w, w_s, w_fmt, first):
            nc.tensor.matmul_mx(
                out=bank[:],
                lhsT=x_w[:, 2 * P * a : 2 * P * (a + 1)].bitcast(E2M1),
                lhsT_scale=x_s[:, P * a : P * (a + 1)],
                rhs=w_w[:].bitcast(w_fmt),
                rhs_scale=w_s,
                start=first,
                stop=not first,
            )

        warm = ps.tile([P, M], F32, name="warm", tag="bank7")
        for rehearsal in range(WARM_PASSES):
            nc.tensor.matmul_mx(
                out=warm[:],
                lhsT=xt_w[:, 0 : 2 * P].bitcast(E2M1),
                lhsT_scale=staged[:, 0:P],
                rhs=xt_w[:].bitcast(E2M1),
                rhs_scale=staged[:, 0:T],
                start=True,
                stop=True,
            )

        q_ps, p_ps, q_sb, th, turned, d_bf, b_ps = {}, {}, {}, {}, {}, {}, {}

        def sums(a):
            q_ps[a] = ps.tile([P, M], F32, name="q_ps%d" % a, tag="bank%d" % a)
            p_ps[a] = ps.tile([P, M], F32, name="p_ps%d" % a, tag="bank%d" % (TILES + a))
            product(q_ps[a], xt_w, xt_s, a, wb_w, wb_s, E4M3, True)
            product(q_ps[a], xq_w, xq_s, a, we_w, we_s, E2M1, False)
            product(p_ps[a], xt_w, xt_s, a, wa_w, wa_s, E4M3, True)
            product(p_ps[a], xq_w, xq_s, a, wc_w, wc_s, E4M3, False)

        def copy_q(a):
            q_sb[a] = sb.tile([P, PACK, P], F32, name="q_sb%d" % a)
            nc.scalar.activation(out=q_sb[a][:], in_=q_ps[a][:].rearrange("t (c j) -> t j c", j=PACK), func=ACT.Copy)

        def tanh_of_gap(a):
            gap = sb.tile([P, PACK, P], F32, name="gap%d" % a)
            nc.vector.tensor_tensor(
                out=gap[:], in0=p_ps[a][:].rearrange("t (c j) -> t j c", j=PACK), in1=q_sb[a][:], op=ALU.subtract
            )
            th[a] = sb.tile([P, PACK, P], F32, name="th%d" % a)
            nc.scalar.activation(out=th[a][:], in_=gap[:], func=ACT.Tanh)

        def turn(a):
            turned[a] = ps.tile([P, PACK, P], F32, name="turned%d" % a, tag="bank%d" % a)
            for j in range(PACK):
                nc.tensor.transpose(turned[a][:, j, :], th[a][:, j, :], ident[:])

        def weigh(a):
            d_bf[a] = sb.tile([P, P, PACK], BF16, name="d_bf%d" % a, align_bytes=64)
            nc.vector.tensor_tensor(
                out=d_bf[a][:],
                in0=turned[a][:].rearrange("p j t -> p t j"),
                in1=us_sb[:].unsqueeze(1).to_broadcast([P, P, PACK]),
                op=ALU.mult,
            )

        def weigh_on_scalar(a):
            d_bf[a] = sb.tile([P, P, PACK], BF16, name="d_bf%d" % a, align_bytes=64)
            for j in range(PACK):
                nc.scalar.activation(
                    out=d_bf[a][:, :, j], in_=turned[a][:, j, :], func=ACT.Copy, scale=us_sb[:, j : j + 1]
                )

        def quantise_d(a):
            nc.vector.quantize_mx(
                out=d_w[:, HALF + P * a : HALF + P * (a + 1)].bitcast(E5M2),
                scales=d_s[:, HALF + P * a : HALF + P * (a + 1)],
                in_=d_bf[a][:].rearrange("p t j -> p (t j)"),
            )

        y = [sb.tile([P, PACK, HALF], F32, name="y%d" % h) for h in range(2)]
        y_bf = sb.tile([P, T, PACK], BF16, name="y_bf", align_bytes=64)
        y_w = sb.tile([P, T], I32, name="y_w", align_bytes=64)
        y_s = sb.tile([P, T], U8, name="y_s", align_bytes=64)
        out_rows = out_0.rearrange("(p i) t -> p i t", i=PACK)

        def way_back(h, i):
            b_ps[h, i] = ps.tile([P, T], F32, name="b_ps%d_%d" % (h, i), tag="bank%d" % (TILES * (1 - h) + i))
            nc.tensor.matmul_mx(
                out=b_ps[h, i][:],
                lhsT=wt_wd[:, P * i : P * (i + 1)].bitcast(E4M3),
                lhsT_scale=wt_sd[:, P * i : P * (i + 1)],
                rhs=d_w[:, HALF * h : HALF * h + T].bitcast(E5M2),
                rhs_scale=d_s[:, HALF * h : HALF * h + T],
                start=True,
                stop=True,
            )

        def result(h, i):
            cols = slice(HALF * h, HALF * (h + 1))
            nc.vector.tensor_tensor(out=y[h][:, i, :], in0=b_ps[h, i][:, HALF:T], in1=rw_sb[:, cols], op=ALU.mult)
            if i % 2 == 1:
                nc.sync.dma_start(out=out_rows[:, i - 1 : i + 1, cols], in_=y[h][:, i - 1 : i + 1, :])

        def interleave(copy, h, t0, t1):
            copy(
                out=y_bf[:, HALF * h + t0 : HALF * h + t1, :].rearrange("p (c e) i -> p c i e", e=4),
                in_=y[h][:, :, t0:t1].rearrange("p i (c e) -> p c i e", e=4),
            )

        def quantise_y(h, queue):
            cols = slice(HALF * h, HALF * (h + 1))
            nc.vector.quantize_mx(
                out=y_w[:, cols].bitcast(E4M3),
                scales=y_s[:, cols],
                in_=y_bf[:, cols, :].rearrange("p t i -> p (t i)"),
            )
            queue.dma_start(out=out_1[0].rearrange("p c r -> p (c r)").bitcast(I32)[:, cols], in_=y_w[:, cols])

        sums(0)
        copy_q(0)
        sums(1)
        copy_q(1)
        tanh_of_gap(0)
        deal(wt_wd[:], wt_w[:].bitcast(I32))
        sums(2)
        copy_q(2)
        tanh_of_gap(1)
        deal(wt_sd[:], wt_s[:])
        sums(3)
        copy_q(3)
        tanh_of_gap(2)
        tanh_of_gap(3)
        for a in range(TILES):
            turn(a)
        weigh_on_scalar(2)
        weigh(0)
        weigh(1)
        quantise_d(0)
        quantise_d(1)
        for i in range(PACK):
            way_back(0, i)
        weigh(3)
        result(0, 0)
        quantise_d(3)
        quantise_d(2)
        for i in range(1, PACK):
            result(0, i)
        for i in range(PACK):
            way_back(1, i)
        interleave(nc.scalar.copy, 0, 0, HALF)
        for i in range(PACK):
            result(1, i)
        interleave(nc.scalar.copy, 1, SPLIT, HALF)
        interleave(nc.vector.tensor_copy, 1, 0, SPLIT)
        quantise_y(0, nc.sync)
        quantise_y(1, nc.scalar)
        for q in range(QUADS):
            queue = nc.scalar if q == 0 else nc.sync
            queue.dma_start(
                out=out_2[0, 4 * q : 4 * q + 4, :].bitcast(I32),
                in_=y_s[32 * q : 32 * q + 4, :].bitcast(I32),
            )
